import numpy as np
CORES = [35,38,43,46]
N = 4
R, KR, T = 4096, 32768, 1024
CAPP = 512
def entries(a): return a.T.reshape(-1)
def pack(v, P): return np.ascontiguousarray(np.asarray(v, np.int32).reshape(-1, P).T)
def owners(rng, n, cap):
    return np.stack([rng.permutation(np.repeat(np.arange(N), cap))[:n] for r in range(N)])
def lists(rng, how):
    K = rng.permutation(N * KR)[:N * R]
    G = R * owners(rng, T, CAPP) + rng.integers(0, R, (N, T))
    if how == "uniform": G[:, :T // 8] = -1
    if how == "alike": O = np.stack([np.repeat(rng.permutation(N)[:T // CAPP], CAPP) for r in range(N)]); G = R * O + rng.integers(0, R, N)[O]
    if how == "edge":
        en = np.concatenate([KR * np.arange(N), KR * np.arange(N) + KR - 1]); ep = np.concatenate([R * np.arange(N), R * np.arange(N) + R - 1])
        K = rng.permutation(np.setdiff1d(np.arange(N * KR), en))[:N * R]; K[ep] = rng.permutation(en)
        G = np.concatenate([np.tile(ep, (N, 1)), R * owners(rng, T - 2 * N, CAPP - 2) + rng.integers(0, R, (N, T - 2 * N))], axis=1)
    if how == "full":
        lo = KR * int(rng.integers(N)) + int(rng.integers(T // 2, KR - N * R - T // 2 + 1)); K = lo + rng.permutation(N * R); rp = rng.permutation(N)
        G = np.stack([np.concatenate([R * h + rng.permutation(R)[:CAPP] for h in rp[:T // CAPP]]) for r in range(N)]); G[int(rng.integers(N)), :CAPP] = -1
    if how == "own":
        m = min(32, KR // R); c = int(rng.integers(m)); q = np.stack([rng.permutation(np.concatenate([2 * rng.permutation(KR // (2 * m))[:R // 2], 2 * rng.permutation(KR // (2 * m))[:R // 2] + 1])) for r in range(N)])
        pp = KR * ((np.arange(N) + int(rng.integers(1, N))) % N)[:, None] + m * q
        K = (pp + c).reshape(-1); O = (np.arange(N)[:, None] + 1 + np.arange(T) // 2 % (N - 1)) % N; O[:, :CAPP] = np.arange(N)[:, None]
        ev = np.stack([np.nonzero(v % 2 == 0)[0] for v in q]); G = R * O + ev[O, rng.integers(0, R // 2, (N, T))]; G[:, CAPP::2] = -1
    F = np.setdiff1d(np.arange(N * KR), K); Z = F[rng.integers(0, len(F), (N, T))]
    if how == "full": Z = np.tile(np.where(np.arange(T) % 2 == 0, lo - 1 - np.arange(T) // 2, lo + N * R + np.arange(T) // 2), (N, 1))
    if how == "own": Z = np.take_along_axis(pp, rng.integers(0, R, (N, T)), axis=1) + (c + rng.integers(1, m, (N, T))) % m
    if how == "absent":
        G[:, :T // 3] = -1; G[int(rng.integers(N))] = -1
        for j, d in ((0, 1), (1, -1)): nb = np.intersect1d(K + d, F); Z[:, j::4] = nb[rng.integers(0, len(nb), (N, T // 4))]
    W = np.where(G >= 0, K[np.maximum(G, 0)], Z); W = np.take_along_axis(W, np.argsort(rng.random((N, T)), axis=1), axis=1)
    return {"kb": np.stack([pack(k, 16) for k in K.reshape(N, R)]), "ka": np.stack([pack(w, 16) for w in W])}
def setup_inputs(rng):
    return dict({"tab": rng.standard_normal((N, 128, R), dtype=np.float32)}, **lists(rng, "uniform"))
def setup_inputs_absent(rng):
    d = setup_inputs(rng); d.update(lists(rng, "absent"))
    for k in ("tab",): d[k] = (d[k].astype(np.float32) * 1048576.0).astype(d[k].dtype)
    return d
def setup_inputs_alike(rng):
    d = setup_inputs(rng); d.update(lists(rng, "alike"))
    for k in ("tab",): d[k] = (d[k].astype(np.float32) * (1 / 1024.0)).astype(d[k].dtype)
    return d
def setup_inputs_edge(rng):
    d = setup_inputs(rng); d.update(lists(rng, "edge"))
    return d
def setup_inputs_full(rng):
    d = setup_inputs(rng); d.update(lists(rng, "full"))
    return d
def setup_inputs_own(rng):
    d = setup_inputs(rng); d.update(lists(rng, "own"))
    return d
def check_inputs(x):
    bad = []
    if x["kb"].min() < 0 or x["kb"].max() >= N * KR: bad.append("kb out of range")
    if x["ka"].min() < 0 or x["ka"].max() >= N * KR: bad.append("ka out of range")
    if bad: return bad
    K = np.concatenate([entries(k) for k in x["kb"]]); H = np.full(N * KR, N); H[K] = np.arange(N * R) // R
    if len(np.unique(K)) < N * R: bad.append("a key stands twice in kb")
    if max(int(np.bincount(H[entries(a)], minlength=N + 1)[:N].max()) for a in x["ka"]) > CAPP: bad.append("more than CAPP entries of a list have their columns on one rank")
    return bad
def reference(tab, kb, ka):
    A = np.concatenate(list(tab) + [np.zeros((128, 1), tab.dtype)], axis=1)
    K, Q = np.concatenate([entries(k) for k in kb]), np.stack([entries(q) for q in ka])
    P = np.full(N * KR, N * R); P[K] = np.arange(N * R)
    return {"y": np.stack([A[:, P[Q[r]]] for r in range(N)])}

@@ -1,0 +1,367 @@
+from concourse.bass import DstId, RemoteDMATransfer
+from concourse.mybir import AluOpType as A, ActivationFunctionType as F
+
+NR = 4
+NCORES = 48
+RNG = 16384
+ZC = 16385
+FILL = 16392
+WIN = 17536
+F0 = 1024
+
+SCRATCH = {}
+for _names, _w, _dt in (("win", WIN, "bfloat16"), ("kbi", 256, "int32"), ("kh kl", 64, "int32"), ("kn jt", 64, "float32"),
+                        ("ko", 64, "uint16"), ("kai", 64, "int32"), ("ka1", 64, "float32"), ("qm qx", 256, "uint16"),
+                        ("pidx", 1, "int32"), ("ci", 8, "int32"), ("cf at bias", 8, "float32"), ("col", 16, "float32"),
+                        ("bt", 256, "bfloat16"), ("dat", 1024, "bfloat16"), ("j16 xx", 512, "float32"),
+                        ("m16", 512, "bfloat16"), ("wsel", 8, "bfloat16"), ("got", 4096, "bfloat16"),
+                        ("wb wv ff pd selr", 32, "float32"), ("pin", 96, "float32"), ("cii", 32, "int32"),
+                        ("cidx so", 32, "uint16"), ("k32 kk pmt fn cn kf", 32, "bfloat16"),
+                        ("rj pj mask8 r16 pi pm xm", 128, "float32"),
+                        ("blk nblk upp eye dgo", 128, "bfloat16"), ("selh", 256, "float32"), ("w2", 2048, "float32"),
+                        ("tl", 128, "uint16"), ("tabs", 4096, "float32"),
+                        ("snd", 2048, "float32"), ("land", 2056, "float32"), ("fl", 64, "uint16"), ("ys", 1024, "float32")):
+    for _n in _names.split():
+        SCRATCH[_n] = ("sbuf", [128, _w], _dt)
+for _n in ("psw", "pso", "psx", "psl", "psf"):
+    SCRATCH[_n] = ("psum", [128, 512], "float32")
+NEV = 128
+SEMAPHORES = ["e%d" % i for i in range(NEV)] + [k + str(i) for k in ("rq", "rp", "rd") for i in range(NR)] + [
+    "kq", "qr", "pp", "lk", "lq", "lr", "lp", "ld", "lw"]
+
+
+def event(sem=None, total=0):
+    return {"sem": sem, "total": total, "used": False, "known": []}
+
+
+def run_schedule(ops, queues, T):
+    know = {q: [] for q in queues}
+    plan = []
+    for op in ops:
+        kn = know[op["q"]]
+        waits = []
+        for d in op["deps"]:
+            if any(d is k for k in kn):
+                continue
+            waits.append(d)
+            d["used"] = True
+            for k in [d] + d["known"]:
+                if not any(k is x for x in kn):
+                    kn.append(k)
+        if op["ev"] is not None:
+            op["ev"]["known"].extend(kn)
+            op["ev"]["total"] += op["n"]
+        plan.append(waits)
+    n = 0
+    for op in ops:
+        ev = op["ev"]
+        if ev is not None and ev["used"] and ev["sem"] is None:
+            ev["sem"] = T.sem["e%d" % n]
+            n += 1
+    for op, waits in zip(ops, plan):
+        for d in waits:
+            queues[op["q"]].wait_ge(d["sem"], d["total"])
+        if op["fn"] is None:
+            continue
+        ins = op["fn"]()
+        if op["ev"] is not None and op["ev"]["used"]:
+            ins.then_inc(op["ev"]["sem"], op["n"])
+
+
+def bits(m):
+    return bin(m).count("1")
+
+
+def low_bits(m, lo, hi):
+    e = [i for i in range(m.bit_length()) if m >> i & 1]
+    return sum(1 << i for i in e[lo:hi])
+
+
+def rank_program(g, core, T, topo):
+    team = None
+    for r in range(NR):
+        c0 = T.cores[r]
+        if topo.chip(core) == topo.chip(c0) and topo.die(core) == topo.die(c0):
+            s, team = r, [c0] + [c for c in range(NCORES) if c != c0 and topo.chip(c) == topo.chip(c0) and topo.die(c) == topo.die(c0)]
+    if team is None:
+        return
+    part = team.index(core)
+    rank = part == 0
+    V, S = g.vector, g.scalar
+    ops = []
+
+    def do(q, fn, deps=(), ev=None, n=1):
+        e = ev if ev is not None else event()
+        ops.append({"q": q, "fn": fn, "deps": list(deps), "ev": e, "n": n})
+        return e
+
+    def plain(q, fn, deps=()):
+        ops.append({"q": q, "fn": fn, "deps": list(deps), "ev": None, "n": 0})
+
+    def act(out, in_, func, bias=0.0, scale=1.0, deps=()):
+        return do("s", lambda: S.activation(out, in_, func, bias=bias, scale=scale), deps)
+
+    def ts(out, in0, s1, s2, op0, op1=None, deps=()):
+        if op1 is None:
+            return do("v", lambda: V.tensor_scalar(out, in0, s1, None, op0), deps)
+        return do("v", lambda: V.tensor_scalar(out, in0, s1, s2, op0, op1), deps)
+
+    def tt(out, a, b, op, deps=()):
+        return do("v", lambda: V.tensor_tensor(out, a, b, op), deps)
+
+    def vcopy(out, in_, deps=()):
+        return do("v", lambda: V.tensor_copy(out, in_), deps)
+
+    def fill(ap, deps=(), ev=None):
+        return do("v", lambda: V.memset(ap, 0.0), deps, ev)
+
+    def iota(out, pattern, base, cm, integer=False, ev=None):
+        if integer:
+            return do("g", lambda: g.iota(out, pattern, base, cm), (), ev)
+        return do("g", lambda: g.iota(out, pattern, base, cm, allow_small_or_imprecise_dtypes=True), (), ev)
+
+    def mm(out, lhsT, rhs, start, stop, deps=(), ev=None):
+        return do("t", lambda: g.tensor.matmul(out, lhsT, rhs, start, stop), deps, ev)
+
+    def dma(out, in_, deps=(), ev=None, q="y"):
+        return do(q, lambda: (S if q == "s" else g.sync).dma_start(out, in_), deps, ev, 16)
+
+    def fused(tr, lsem, deps):
+        def issue():
+            xs = []
+            for m, rsem, src, dst, cores in tr:
+                ids = [topo.addr(c) for c in cores]
+                xs.append(RemoteDMATransfer(dst_ids=[DstId(rid=i[0], pnc=i[1]) for i in ids], dma_engine_mask=m,
+                                            remote_sem=rsem, srcs=[src], dsts=[dst for _ in cores]))
+            return g.remote_dma_fused(xs, local_sem=lsem)
+        plain("g", issue, deps)
+
+    if rank:
+        peers = [r for r in range(NR) if r != s]
+        far = [r for r in peers if topo.chip(T.cores[r]) != topo.chip(core)]
+        near = [r for r in peers if topo.chip(T.cores[r]) == topo.chip(core)]
+        assert all(topo.may_write(core, T.cores[r]) for r in peers)
+        fmask = topo.mask(core, T.cores[far[0]])
+        nmask = topo.mask(core, T.cores[near[0]]) & ~fmask
+        nin = {r: bits(fmask if r in far else nmask) for r in peers}
+
+        def share(ap, rsem, lsem, deps):
+            fused([(m, rsem, ap, ap, [T.cores[r] for r in rs]) for rs, m in ((far, fmask), (near, nmask))], lsem, deps)
+    tmask = topo.mask(team[0], team[1])
+
+    e_kb, e_ka = event(), event()
+    if rank:
+        for t, src, ev in ((T.kbi, T.kb, e_kb), (T.kai, T.ka, e_ka)):
+            for gr in range(8):
+                dma(t[16 * gr:16 * gr + 16, :], src[:, :], ev=ev, q="ys"[gr % 2])
+    else:
+        e_kb = event(T.sem.kq, 4)
+
+    f_0 = fill(T.win[:, 0:F0])
+    i_p = iota(T.pidx[:], [[0, 1]], 0, 1, True)
+    i_a = iota(T.at[:, 0:4], [[1, 4]], 1 + 4 * part, 0)
+    i_j = iota(T.jt[:], [[16, 64]], ZC, 1)
+    i_b = iota(T.bt[:], [[1, 256]], 1, 0)
+    if rank:
+        fused([(low_bits(tmask, 4 * j - 4, 4 * j), T.sem.kq, T.kbi[:, 64 * j:64 * j + 64], T.kbi[:, 0:64], [team[j]]) for j in (1, 2, 3)],
+              T.sem.lk, [e_kb])
+
+    F1 = F0 + (5 if rank else 6) * F0
+    F2 = F1 + (2 if rank else 3) * F0
+    F3 = F2 + (1 if rank else 2) * F0
+    f_d = event()
+    for c in range(F1, F2, F0):
+        dma(T.win[:, c:c + F0], T.win[:, 0:F0], [f_0], f_d)
+    f_a = [act(T.win[:, c:c + F0], T.win[:, 0:F0], F.Copy, deps=[f_0]) for c in range(F0, F1, F0)]
+    f_v = event()
+    vb = [F3 + 8 * ((FILL - F3) // 8 * k // 4) for k in range(4)] + [FILL]
+
+    def vfill(k):
+        fill(T.win[:, vb[k]:vb[k + 1]], ev=f_v)
+
+    LANE, GRP, ODD, RQ, H = range(5)
+    QM1, EV, ORDP, WT, W0, W1 = range(6)
+    SH, AND, SUB = A.arith_shift_right, A.bitwise_and, A.subtract
+    d = [ts(T.ci[:, k:k + 1], T.pidx[:], a, b, o1, o2, [i_p]) for k, a, b, o1, o2 in (
+        (GRP, 4, None, SH, None), (LANE, 15, None, AND, None), (ODD, 1, None, AND, None),
+        (RQ, 4, 3, SH, AND), (H, 6, None, SH, None))]
+    if not rank:
+        vfill(0)
+    e_cf = vcopy(T.cf[:, 0:5], T.ci[:, 0:5], d)
+
+    def fc(k):
+        return T.cf[:, k:k + 1]
+
+    def cc(k):
+        return T.col[:, k:k + 1]
+
+    e_ev = ts(cc(EV), fc(ODD), -1.0, 1.0, A.mult, A.add, [e_cf])
+    if rank:
+        e_qm = ts(cc(QM1), fc(GRP), float(RNG), -1.0, A.mult, A.add, [e_cf])
+        e_bias = ts(T.bias[:, 0:4], T.at[:, 0:4], fc(ODD), None, A.mult, deps=[e_cf, i_a])
+        qlo = T.qm[:, 64 * s:64 * s + 64]
+        e = ts(T.ka1[:], T.kai[:], cc(QM1), 0.0, SUB, A.max, [e_ka, e_qm])
+        vfill(0)
+        e_ql = ts(qlo, T.ka1[:], float(ZC), None, A.min, deps=[e])
+        share(qlo, T.sem["rq%d" % s], T.sem.lq, [e_ql])
+        q_in = {r: event(T.sem["rq%d" % r], nin[r]) for r in peers}
+        q_in[s] = e_ql
+        vfill(1)
+    else:
+        e_bias = ts(T.bias[:, 0:4], T.at[:, 0:4], fc(ODD), None, A.mult, deps=[e_cf, i_a])
+        vfill(1)
+        vfill(2)
+    f_g = iota(T.win[:, F2:F3], [[0, F3 - F2]], 0, 0)
+
+    def values(a):
+        return ts(T.dat[:, 256 * a:256 * a + 256], T.bt[:], cc(EV), T.bias[:, a:a + 1], A.mult, A.add, [e_ev, e_bias, i_b])
+
+    e_dat = []
+    if not rank:
+        e_dat = [values(a) for a in range(4)]
+        vfill(3)
+    e1 = ts(T.kh[:], T.kbi[:, 0:64], 14, None, SH, deps=[e_kb])
+    e2 = ts(T.kl[:], T.kbi[:, 0:64], RNG - 1, None, AND, deps=[e_kb])
+    if rank:
+        e_dat.append(values(0))
+    e = ts(T.kn[:], T.kh[:], fc(GRP), None, A.not_equal, deps=[e1, e_cf])
+    if rank:
+        e_dat.append(values(1))
+    e = tt(T.kn[:], T.kn[:], T.jt[:], A.mult, [e, i_j])
+    if rank:
+        e_dat.append(values(2))
+    e = tt(T.kn[:], T.kn[:], T.kl[:], A.max, [e, e2])
+    if rank:
+        e_dat.append(values(3))
+    e_ko = ts(T.ko[:], T.kn[:], 1.0, None, A.add, deps=[e])
+    if rank:
+        vfill(2)
+        e_q = [vcopy(T.qx[:, r::4], T.qm[:, 64 * r:64 * r + 64], [q_in[r]]) for r in [s] + near + far]
+        fused([(tmask, T.sem.qr, T.qx[:], T.qx[:], team[1:])], T.sem.lr, e_q)
+        e_tab = dma(T.tabs[:, :], T.tab[:, :], e_q)
+        vfill(3)
+    else:
+        e_q = [event(T.sem.qr, bits(tmask))]
+    e_dir = vcopy(T.win[:, 0:WIN].indirect(T.ko[:, 0:64]), T.dat[:], [f_0, f_d, f_g, f_v, e_ko] + f_a + e_dat)
+
+    e = act(cc(WT), fc(LANE), F.Abs, -1.0, 1.0, [e_cf])
+    e0 = act(cc(W0), fc(LANE), F.Relu, 1.0, -1.0, [e_cf])
+    e1 = act(cc(W1), cc(WT), F.Relu, 256.0, -256.0, [e])
+    e_ws = act(T.wsel[:, 0:1], cc(W0), F.Identity, cc(W1), 1.0, [e0, e1])
+
+    if rank:
+        i_16 = iota(T.j16[:], [[0, 32], [1, 16]], 0, 0)
+        i_rj = iota(T.rj[:], [[0, 2], [1, 4], [0, 16]], 0, 0)
+        i_pj = iota(T.pj[:], [[-1, 128]], 0, 1)
+        i_k = iota(T.k32[:], [[32, 32]], 0, 0)
+        i_kk = iota(T.kk[:], [[32, 32]], 512, 0)
+        e = act(T.j16[:], T.j16[:], F.Abs, fc(LANE), -1.0, [i_16, e_cf])
+        e_m16 = act(T.m16[:], T.j16[:], F.Relu, 1.0, -1.0, [e])
+        e = act(T.rj[:], T.rj[:], F.Abs, fc(RQ), -1.0, [i_rj, e_cf])
+        e_op = act(cc(ORDP), fc(H), F.Identity, fc(LANE), 16.0, [e_cf])
+        e_bl = act(T.blk[:], T.rj[:], F.Relu, 1.0, -1.0, [e])
+        e = act(T.pj[:], T.pj[:], F.Abs, deps=[i_pj])
+        e_nb = act(T.nblk[:], T.blk[:], F.Copy, 0.0, -1.0, [e_bl])
+        e_eye = act(T.eye[:], T.pj[:], F.Relu, 1.0, -1.0, [e])
+        e_pt = act(T.pmt[:], T.k32[:], F.Identity, cc(ORDP), 0.0, [i_k, e_op])
+        e_dg = act(T.dgo[:], T.eye[:], F.Copy, 0.0, cc(ORDP), [e_eye, e_op])
+        i_ci = iota(T.cii[:], [[1, 32]], 0, 0, True)
+        z_w2 = iota(T.w2[:, 0:512], [[0, 512]], 0, 0)
+        e_up = do("g", lambda: g.affine_select(T.upp[:], T.blk[:], [[-1, 128]], A.is_ge, 0.0, 0, 1), [e_bl])
+        i_r = iota(T.selr[:], [[0, 8], [1, 4]], 0, 0)
+        i_bi = iota(T.mask8[:], [[0, 4], [1, 8], [0, 4]], 0, 0)
+        i_i = iota(T.r16[:], [[0, 8], [1, 16]], 0, 0)
+        i_pi = iota(T.pi[:], [[0, 8], [-1, 16]], 0, 1)
+
+    e_w = event()
+    for n in range(8):
+        win = T.win[:, 0:ZC + 1].indirect(T.qx[:, 32 * n:32 * n + 32])
+        o = T.got[:, 512 * n:512 * n + 512]
+        dep = [e_dir] + e_q
+        e = vcopy(o, win, dep) if n % 2 == 0 else act(o, win, F.Copy, deps=dep)
+        for k in range(4 * n, 4 * n + 4):
+            mm(T.psw[:, k:k + 1], T.got[:, 128 * k:128 * k + 128], T.wsel[:, 0:1], True, True, [e, e_ws], e_w)
+
+    queues = {"g": g, "v": V, "s": S, "y": g.sync, "t": g.tensor}
+    if not rank:
+        e = vcopy(T.wb[:], T.psw[:, 0:32], [e_w])
+        rid, pid, _ = topo.addr(team[0])
+        m = low_bits(topo.mask(core, team[0]), 0, 8)
+        plain("g", lambda: g.remote_dma(T.pin[:, 32 * part - 32:32 * part], T.wb[:], T.sem.pp, T.sem.lw, pid=pid, routing_id=rid,
+                                        dma_engine_mask=m), [e])
+        plain("g", None, [event(T.sem.lw, 8)])
+        run_schedule(ops, queues, T)
+        return
+
+    e = act(T.selr[:], T.selr[:], F.Abs, fc(RQ), -1.0, [i_r])
+    e_bi = act(T.mask8[:], T.mask8[:], F.Abs, fc(GRP), -1.0, [i_bi])
+    e_ii = act(T.r16[:], T.r16[:], F.Abs, fc(LANE), -1.0, [i_i])
+    e_selr = act(T.selr[:], T.selr[:], F.Relu, 1.0, -1.0, [e])
+    e_m8 = act(T.mask8[:], T.mask8[:], F.Relu, 1.0, -1.0, [e_bi])
+    e_r16 = act(T.r16[:], T.r16[:], F.Relu, 1.0, -1.0, [e_ii])
+    po = T.pso[:, 0:32]
+    mm(po, T.eye[:], T.k32[:], True, False, [e_eye, i_k])
+    mm(po, T.eye[:], T.pmt[:], False, False, [e_pt])
+    z_ld = fill(T.land[:, 2048:2056])
+    e_ci = vcopy(T.cidx[:], T.cii[:], [i_ci])
+    e_sh = [ts(T.selh[:, 128 * h:128 * h + 128], T.pi[:], float(16 * (4 * h + s)), None, A.is_equal, deps=[i_pi]) for h in range(2)]
+
+    e_pp = event(T.sem.pp, 3 * 8)
+    eb = tt(T.wb[:], T.pin[:, 32:64], T.pin[:, 64:96], A.add, [e_pp])
+    ea = tt(T.wv[:], T.psw[:, 0:32], T.pin[:, 0:32], A.add, [e_pp, e_w])
+    e_wv = tt(T.wv[:], T.wv[:], T.wb[:], A.add, [ea, eb])
+    e_fn = ts(T.fn[:], T.wv[:], 0.0, None, A.is_equal, deps=[e_wv])
+    e_cn = do("v", lambda: V.tensor_tensor_scan(T.cn[:], T.fn[:], T.fn[:], 0.0, A.add, A.max), [e_fn])
+    e_kf = tt(T.kf[:], T.kk[:], T.fn[:], A.mult, [i_kk, e_fn])
+    e_x = tt(T.xx[:], T.wv[:, 0:32].indirect(T.cidx[:, 0:32]), T.m16[:], A.mult, [e_wv, e_ci, e_m16])
+    mm(po, T.dgo[:], T.fn[:], False, False, [e_dg, e_fn])
+    mm(po, T.upp[:], T.fn[:], False, False, [e_up])
+    mm(po, T.nblk[:], T.cn[:], False, False, [e_nb, e_cn])
+    e_z = mm(po, T.eye[:], T.kf[:], False, True, [e_kf])
+    e_so = vcopy(T.so[:], po, [e_z])
+    e_ff = ts(T.ff[:], T.fn[:], -1.0, 1.0, A.mult, A.add, [e_fn])
+    e_w2 = vcopy(T.w2[:, 0:2048].indirect(T.so[:, 0:32]), T.xx[:], [e_so, e_x, z_w2])
+    e = ts(T.pd[:], T.so[:], float(512 * s - 2048), None, A.add, deps=[e_so])
+    pmo = T.pm[:, 32 * s:32 * s + 32]
+    e_pm = tt(pmo, T.pd[:], T.ff[:], A.mult, [e, e_ff])
+    share(pmo, T.sem["rp%d" % s], T.sem.lp, [e_pm])
+    e_x = [mm(T.psx[:, 32 * k:32 * k + 32], T.w2[:, 128 * k:128 * k + 128], T.selr[:], True, True, [e_w2, e_selr]) for k in range(4)]
+    e = tt(T.xm[:], T.psx[:, 0:128], T.mask8[:], A.mult, e_x + [e_m8])
+    e_l = mm(T.psl[:, 0:128], T.r16[:], T.xm[:], True, True, [e, e_r16])
+    e_tl = {r: ts(T.tl[:, 32 * r:32 * r + 32], T.psl[:, r:128:4], -257.0, 0.0, A.add, A.max, [e_l]) for r in far[::-1] + near + [s]}
+
+    land = T.land[:, 512 * s:512 * s + 512]
+    out = {r: T.snd[:, 512 * r:512 * r + 512] for r in peers}
+    out[s] = land
+    e_col = {}
+    for r, eng in ((far[1], "s"), (far[0], "v"), (near[0], "v"), (s, "s")):
+        w = T.tabs[:, :].indirect(T.tl[:, 32 * r:32 * r + 32])
+        dep = [e_tl[r], e_tab]
+        e_col[r] = vcopy(out[r], w, dep) if eng == "v" else act(out[r], w, F.Copy, deps=dep)
+    for r in far + near:
+        rid, pid, _ = topo.addr(T.cores[r])
+        plain("g", lambda r=r, rid=rid, pid=pid: g.remote_dma(
+            land, out[r], T.sem["rd%d" % s], T.sem.ld, pid=pid, routing_id=rid, dma_engine_mask=fmask if r in far else nmask), [e_col[r]])
+
+    order = [s] + near + far
+    p_in = {r: event(T.sem["rp%d" % r], nin[r]) for r in peers}
+    p_in[s] = e_pm
+    e_f = []
+    for h in range(2):
+        for n, r in enumerate(order):
+            e = mm(T.psf[:, 32 * h:32 * h + 32], T.selh[:, 128 * h:128 * h + 128], T.pm[:, 32 * r:32 * r + 32], n == 0, n == 3, [e_sh[h], p_in[r]])
+        e_f.append(e)
+    e_fl = [ts(T.fl[:, h::2], T.psf[:, 32 * h:32 * h + 32], 2048.0, None, A.add, deps=e_f) for h in range(2)]
+    d_in = [event(T.sem["rd%d" % r], nin[r]) for r in peers]
+    e_y = event()
+    for k in range(4):
+        w = T.land[:, 0:2049].indirect(T.fl[:, 16 * k:16 * k + 16])
+        o = T.ys[:, 256 * k:256 * k + 256]
+        dep = e_fl + [e_col[s], z_ld] + d_in
+        e = vcopy(o, w, dep) if k % 2 == 0 else act(o, w, F.Copy, deps=dep)
+        dma(T.y[:, 256 * k:256 * k + 256], o, [e], e_y)
+    plain("y", None, [e_y])
+    n = bits(fmask) + bits(nmask)
+    plain("g", None, [event(T.sem.lk, 12), event(T.sem.lq, n), event(T.sem.lr, bits(tmask)), event(T.sem.lp, n),
+                      event(T.sem.ld, n + bits(fmask))])
+    run_schedule(ops, queues, T)

@@ -98,19 +98,19 @@ def rank_program(g, core, T, topo):
     def plain(q, fn, deps=()):
         ops.append({"q": q, "fn": fn, "deps": list(deps), "ev": None, "n": 0})
 
-    def act(out, in_, func, bias=0.0, scale=1.0, deps=()):
-        return do("s", lambda: S.activation(out, in_, func, bias=bias, scale=scale), deps)
+    def act(out, in_, func, bias=0.0, scale=1.0, deps=(), ev=None):
+        return do("s", lambda: S.activation(out, in_, func, bias=bias, scale=scale), deps, ev)
 
-    def ts(out, in0, s1, s2, op0, op1=None, deps=()):
+    def ts(out, in0, s1, s2, op0, op1=None, deps=(), ev=None):
         if op1 is None:
-            return do("v", lambda: V.tensor_scalar(out, in0, s1, None, op0), deps)
-        return do("v", lambda: V.tensor_scalar(out, in0, s1, s2, op0, op1), deps)
+            return do("v", lambda: V.tensor_scalar(out, in0, s1, None, op0), deps, ev)
+        return do("v", lambda: V.tensor_scalar(out, in0, s1, s2, op0, op1), deps, ev)
 
     def tt(out, a, b, op, deps=()):
         return do("v", lambda: V.tensor_tensor(out, a, b, op), deps)
 
-    def vcopy(out, in_, deps=()):
-        return do("v", lambda: V.tensor_copy(out, in_), deps)
+    def vcopy(out, in_, deps=(), ev=None):
+        return do("v", lambda: V.tensor_copy(out, in_), deps, ev)
 
     def fill(ap, deps=(), ev=None):
         return do("v", lambda: V.memset(ap, 0.0), deps, ev)
@@ -166,28 +166,32 @@ def rank_program(g, core, T, topo):
         fused([(low_bits(tmask, 4 * j - 4, 4 * j), T.sem.kq, T.kbi[:, 64 * j:64 * j + 64], T.kbi[:, 0:64], [team[j]]) for j in (1, 2, 3)],
               T.sem.lk, [e_kb])
 
-    F1 = F0 + (5 if rank else 6) * F0
-    F2 = F1 + (2 if rank else 3) * F0
-    F3 = F2 + (1 if rank else 2) * F0
-    f_d = event()
+    F1 = F0 + (7 if rank else 5) * F0
+    F2 = F1 + (1 if rank else 3) * F0
+    F3 = F2 + 2 * F0
+    f_d, f_a, f_g, f_v = event(), event(), event(), event()
     for c in range(F1, F2, F0):
         dma(T.win[:, c:c + F0], T.win[:, 0:F0], [f_0], f_d)
-    f_a = [act(T.win[:, c:c + F0], T.win[:, 0:F0], F.Copy, deps=[f_0]) for c in range(F0, F1, F0)]
-    f_v = event()
+    for c in range(F0, F1, F0):
+        act(T.win[:, c:c + F0], T.win[:, 0:F0], F.Copy, deps=[f_0], ev=f_a)
     vb = [F3 + 8 * ((FILL - F3) // 8 * k // 4) for k in range(4)] + [FILL]
 
     def vfill(k):
         fill(T.win[:, vb[k]:vb[k + 1]], ev=f_v)
 
+    def gfill(k):
+        iota(T.win[:, F2 + F0 * k:F2 + F0 * k + F0], [[0, F0]], 0, 0, ev=f_g)
+
     LANE, GRP, ODD, RQ, H = range(5)
     QM1, EV, ORDP, WT, W0, W1 = range(6)
     SH, AND, SUB = A.arith_shift_right, A.bitwise_and, A.subtract
-    d = [ts(T.ci[:, k:k + 1], T.pidx[:], a, b, o1, o2, [i_p]) for k, a, b, o1, o2 in (
-        (GRP, 4, None, SH, None), (LANE, 15, None, AND, None), (ODD, 1, None, AND, None),
-        (RQ, 4, 3, SH, AND), (H, 6, None, SH, None))]
+    e_c = event()
+    for k, a, b, o1, o2 in ((GRP, 4, None, SH, None), (LANE, 15, None, AND, None), (ODD, 1, None, AND, None),
+                            (RQ, 4, 3, SH, AND), (H, 6, None, SH, None)):
+        ts(T.ci[:, k:k + 1], T.pidx[:], a, b, o1, o2, [i_p], e_c)
     if not rank:
         vfill(0)
-    e_cf = vcopy(T.cf[:, 0:5], T.ci[:, 0:5], d)
+    e_cf = vcopy(T.cf[:, 0:5], T.ci[:, 0:5], [e_c])
 
     def fc(k):
         return T.cf[:, k:k + 1]
@@ -195,54 +199,47 @@ def rank_program(g, core, T, topo):
     def cc(k):
         return T.col[:, k:k + 1]
 
+    e_qm = ts(cc(QM1), fc(GRP), float(RNG), -1.0, A.mult, A.add, [e_cf])
     e_ev = ts(cc(EV), fc(ODD), -1.0, 1.0, A.mult, A.add, [e_cf])
+    e_bias = ts(T.bias[:, 0:4], T.at[:, 0:4], fc(ODD), None, A.mult, deps=[e_cf, i_a])
     if rank:
-        e_qm = ts(cc(QM1), fc(GRP), float(RNG), -1.0, A.mult, A.add, [e_cf])
-        e_bias = ts(T.bias[:, 0:4], T.at[:, 0:4], fc(ODD), None, A.mult, deps=[e_cf, i_a])
         qlo = T.qm[:, 64 * s:64 * s + 64]
         e = ts(T.ka1[:], T.kai[:], cc(QM1), 0.0, SUB, A.max, [e_ka, e_qm])
-        vfill(0)
         e_ql = ts(qlo, T.ka1[:], float(ZC), None, A.min, deps=[e])
         share(qlo, T.sem["rq%d" % s], T.sem.lq, [e_ql])
         q_in = {r: event(T.sem["rq%d" % r], nin[r]) for r in peers}
         q_in[s] = e_ql
-        vfill(1)
     else:
-        e_bias = ts(T.bias[:, 0:4], T.at[:, 0:4], fc(ODD), None, A.mult, deps=[e_cf, i_a])
         vfill(1)
+        gfill(1)
+    gfill(0)
+
+    e_dat = event()
+    for a in range(4):
+        ts(T.dat[:, 256 * a:256 * a + 256], T.bt[:], cc(EV), T.bias[:, a:a + 1], A.mult, A.add, [e_ev, e_bias, i_b], e_dat)
+    if rank:
+        vfill(0)
+        vfill(1)
+        e_q = [vcopy(T.qx[:, r::4], T.qm[:, 64 * r:64 * r + 64], [q_in[r]]) for r in [s] + near + far]
+        fused([(tmask, T.sem.qr, T.qx[:], T.qx[:], team[1:])], T.sem.lr, e_q)
+        e_lr = event(T.sem.lr, bits(tmask))
+        e_tab = dma(T.tabs[:, :], T.tab[:, :], [e_lr])
+        gfill(1)
+    else:
+        e_q = [event(T.sem.qr, bits(tmask))]
         vfill(2)
-    f_g = iota(T.win[:, F2:F3], [[0, F3 - F2]], 0, 0)
-
-    def values(a):
-        return ts(T.dat[:, 256 * a:256 * a + 256], T.bt[:], cc(EV), T.bias[:, a:a + 1], A.mult, A.add, [e_ev, e_bias, i_b])
-
-    e_dat = []
-    if not rank:
-        e_dat = [values(a) for a in range(4)]
         vfill(3)
     e1 = ts(T.kh[:], T.kbi[:, 0:64], 14, None, SH, deps=[e_kb])
     e2 = ts(T.kl[:], T.kbi[:, 0:64], RNG - 1, None, AND, deps=[e_kb])
-    if rank:
-        e_dat.append(values(0))
     e = ts(T.kn[:], T.kh[:], fc(GRP), None, A.not_equal, deps=[e1, e_cf])
     if rank:
-        e_dat.append(values(1))
+        vfill(2)
     e = tt(T.kn[:], T.kn[:], T.jt[:], A.mult, [e, i_j])
     if rank:
-        e_dat.append(values(2))
-    e = tt(T.kn[:], T.kn[:], T.kl[:], A.max, [e, e2])
-    if rank:
-        e_dat.append(values(3))
-    e_ko = ts(T.ko[:], T.kn[:], 1.0, None, A.add, deps=[e])
-    if rank:
-        vfill(2)
-        e_q = [vcopy(T.qx[:, r::4], T.qm[:, 64 * r:64 * r + 64], [q_in[r]]) for r in [s] + near + far]
-        fused([(tmask, T.sem.qr, T.qx[:], T.qx[:], team[1:])], T.sem.lr, e_q)
-        e_tab = dma(T.tabs[:, :], T.tab[:, :], e_q)
         vfill(3)
-    else:
-        e_q = [event(T.sem.qr, bits(tmask))]
-    e_dir = vcopy(T.win[:, 0:WIN].indirect(T.ko[:, 0:64]), T.dat[:], [f_0, f_d, f_g, f_v, e_ko] + f_a + e_dat)
+    e = tt(T.kn[:], T.kn[:], T.kl[:], A.max, [e, e2])
+    e_ko = ts(T.ko[:], T.kn[:], 1.0, None, A.add, deps=[e])
+    e_dir = vcopy(T.win[:, 0:WIN].indirect(T.ko[:, 0:64]), T.dat[:], [f_0, f_d, f_g, f_v, f_a, e_ko, e_dat])
 
     e = act(cc(WT), fc(LANE), F.Abs, -1.0, 1.0, [e_cf])
     e0 = act(cc(W0), fc(LANE), F.Relu, 1.0, -1.0, [e_cf])
@@ -273,23 +270,30 @@ def rank_program(g, core, T, topo):
         i_i = iota(T.r16[:], [[0, 8], [1, 16]], 0, 0)
         i_pi = iota(T.pi[:], [[0, 8], [-1, 16]], 0, 1)
 
-    e_w = event()
+    e_w = [event(), event()]
+    half = [T.psw, T.psw if rank else T.psx]
+
+    def partial(b):
+        e = vcopy(T.wb[:, 16 * b:16 * b + 16], half[b][:, 16 * b:16 * b + 16], [e_w[b]])
+        rid, pid, _ = topo.addr(team[0])
+        m = low_bits(topo.mask(core, team[0]), 0, 8)
+        plain("g", lambda: g.remote_dma(T.pin[:, 32 * part - 32 + 16 * b:32 * part - 16 + 16 * b], T.wb[:, 16 * b:16 * b + 16],
+                                        T.sem.pp, T.sem.lw, pid=pid, routing_id=rid, dma_engine_mask=m), [e])
+
     for n in range(8):
         win = T.win[:, 0:ZC + 1].indirect(T.qx[:, 32 * n:32 * n + 32])
         o = T.got[:, 512 * n:512 * n + 512]
         dep = [e_dir] + e_q
         e = vcopy(o, win, dep) if n % 2 == 0 else act(o, win, F.Copy, deps=dep)
         for k in range(4 * n, 4 * n + 4):
-            mm(T.psw[:, k:k + 1], T.got[:, 128 * k:128 * k + 128], T.wsel[:, 0:1], True, True, [e, e_ws], e_w)
+            mm(half[n // 4][:, k:k + 1], T.got[:, 128 * k:128 * k + 128], T.wsel[:, 0:1], True, True, [e, e_ws], e_w[n // 4])
+        if n == 4 and not rank:
+            partial(0)
 
     queues = {"g": g, "v": V, "s": S, "y": g.sync, "t": g.tensor}
     if not rank:
-        e = vcopy(T.wb[:], T.psw[:, 0:32], [e_w])
-        rid, pid, _ = topo.addr(team[0])
-        m = low_bits(topo.mask(core, team[0]), 0, 8)
-        plain("g", lambda: g.remote_dma(T.pin[:, 32 * part - 32:32 * part], T.wb[:], T.sem.pp, T.sem.lw, pid=pid, routing_id=rid,
-                                        dma_engine_mask=m), [e])
-        plain("g", None, [event(T.sem.lw, 8)])
+        partial(1)
+        plain("g", None, [event(T.sem.lw, 16)])
         run_schedule(ops, queues, T)
         return
 
@@ -304,11 +308,13 @@ def rank_program(g, core, T, topo):
     mm(po, T.eye[:], T.pmt[:], False, False, [e_pt])
     z_ld = fill(T.land[:, 2048:2056])
     e_ci = vcopy(T.cidx[:], T.cii[:], [i_ci])
-    e_sh = [ts(T.selh[:, 128 * h:128 * h + 128], T.pi[:], float(16 * (4 * h + s)), None, A.is_equal, deps=[i_pi]) for h in range(2)]
+    e_sh = event()
+    for h in range(2):
+        ts(T.selh[:, 128 * h:128 * h + 128], T.pi[:], float(16 * (4 * h + s)), None, A.is_equal, deps=[i_pi], ev=e_sh)
 
-    e_pp = event(T.sem.pp, 3 * 8)
+    e_pp = event(T.sem.pp, 3 * 2 * 8)
     eb = tt(T.wb[:], T.pin[:, 32:64], T.pin[:, 64:96], A.add, [e_pp])
-    ea = tt(T.wv[:], T.psw[:, 0:32], T.pin[:, 0:32], A.add, [e_pp, e_w])
+    ea = tt(T.wv[:], T.psw[:, 0:32], T.pin[:, 0:32], A.add, [e_pp] + e_w)
     e_wv = tt(T.wv[:], T.wv[:], T.wb[:], A.add, [ea, eb])
     e_fn = ts(T.fn[:], T.wv[:], 0.0, None, A.is_equal, deps=[e_wv])
     e_cn = do("v", lambda: V.tensor_tensor_scan(T.cn[:], T.fn[:], T.fn[:], 0.0, A.add, A.max), [e_fn])
@@ -325,23 +331,34 @@ def rank_program(g, core, T, topo):
     pmo = T.pm[:, 32 * s:32 * s + 32]
     e_pm = tt(pmo, T.pd[:], T.ff[:], A.mult, [e, e_ff])
     share(pmo, T.sem["rp%d" % s], T.sem.lp, [e_pm])
-    e_x = [mm(T.psx[:, 32 * k:32 * k + 32], T.w2[:, 128 * k:128 * k + 128], T.selr[:], True, True, [e_w2, e_selr]) for k in range(4)]
-    e = tt(T.xm[:], T.psx[:, 0:128], T.mask8[:], A.mult, e_x + [e_m8])
-    e_l = mm(T.psl[:, 0:128], T.r16[:], T.xm[:], True, True, [e, e_r16])
-    e_tl = {r: ts(T.tl[:, 32 * r:32 * r + 32], T.psl[:, r:128:4], -257.0, 0.0, A.add, A.max, [e_l]) for r in far[::-1] + near + [s]}
+    e_x = event()
+    for k in range(4):
+        mm(T.psx[:, 32 * k:32 * k + 32], T.w2[:, 128 * k:128 * k + 128], T.selr[:], True, True, [e_w2, e_selr], e_x)
+    e = tt(T.xm[:], T.psx[:, 0:128], T.mask8[:], A.mult, [e_x, e_m8])
+    places = ((far[0], T.psl, 0), (far[1], T.psw, 0), (near[0], T.pso, 32), (s, T.pso, 64))
+    e_l = {}
+    for r, ps, c in places:
+        e_l[r] = mm(ps[:, c:c + 32], T.r16[:], T.xm[:, r::4], True, True, [e, e_r16])
 
     land = T.land[:, 512 * s:512 * s + 512]
-    out = {r: T.snd[:, 512 * r:512 * r + 512] for r in peers}
-    out[s] = land
     e_col = {}
-    for r, eng in ((far[1], "s"), (far[0], "v"), (near[0], "v"), (s, "s")):
-        w = T.tabs[:, :].indirect(T.tl[:, 32 * r:32 * r + 32])
-        dep = [e_tl[r], e_tab]
-        e_col[r] = vcopy(out[r], w, dep) if eng == "v" else act(out[r], w, F.Copy, deps=dep)
+    for r, ps, c in places:
+        dep = [e_l[r]] if r in far else [e_l[near[0]], e_l[s]]
+        e_tl = ts(T.tl[:, 32 * r:32 * r + 32], ps[:, c:c + 32], -257.0, 0.0, A.add, A.max, dep)
+        e_col[r] = event()
+        buf = T.land if r == s else T.snd
+        for h in range(2):
+            w = T.tabs[:, :].indirect(T.tl[:, 32 * r + 16 * h:32 * r + 16 * h + 16])
+            o = buf[:, 512 * r + 256 * h:512 * r + 256 * h + 256]
+            if h == 0:
+                vcopy(o, w, [e_tl, e_tab], e_col[r])
+            else:
+                act(o, w, F.Copy, deps=[e_tl, e_tab], ev=e_col[r])
     for r in far + near:
         rid, pid, _ = topo.addr(T.cores[r])
         plain("g", lambda r=r, rid=rid, pid=pid: g.remote_dma(
-            land, out[r], T.sem["rd%d" % s], T.sem.ld, pid=pid, routing_id=rid, dma_engine_mask=fmask if r in far else nmask), [e_col[r]])
+            land, T.snd[:, 512 * r:512 * r + 512], T.sem["rd%d" % s], T.sem.ld, pid=pid, routing_id=rid,
+            dma_engine_mask=fmask if r in far else nmask), [e_col[r]])
 
     order = [s] + near + far
     p_in = {r: event(T.sem["rp%d" % r], nin[r]) for r in peers}
@@ -349,7 +366,7 @@ def rank_program(g, core, T, topo):
     e_f = []
     for h in range(2):
         for n, r in enumerate(order):
-            e = mm(T.psf[:, 32 * h:32 * h + 32], T.selh[:, 128 * h:128 * h + 128], T.pm[:, 32 * r:32 * r + 32], n == 0, n == 3, [e_sh[h], p_in[r]])
+            e = mm(T.psf[:, 32 * h:32 * h + 32], T.selh[:, 128 * h:128 * h + 128], T.pm[:, 32 * r:32 * r + 32], n == 0, n == 3, [e_sh, p_in[r]])
         e_f.append(e)
     e_fl = [ts(T.fl[:, h::2], T.psf[:, 32 * h:32 * h + 32], 2048.0, None, A.add, deps=e_f) for h in range(2)]
     d_in = [event(T.sem["rd%d" % r], nin[r]) for r in peers]
@@ -362,6 +379,5 @@ def rank_program(g, core, T, topo):
         dma(T.y[:, 256 * k:256 * k + 256], o, [e], e_y)
     plain("y", None, [e_y])
     n = bits(fmask) + bits(nmask)
-    plain("g", None, [event(T.sem.lk, 12), event(T.sem.lq, n), event(T.sem.lr, bits(tmask)), event(T.sem.lp, n),
-                      event(T.sem.ld, n + bits(fmask))])
+    plain("g", None, [event(T.sem.lk, 12), event(T.sem.lq, n), e_lr, event(T.sem.lp, n), event(T.sem.ld, n + bits(fmask))])
     run_schedule(ops, queues, T)

from concourse.bass import DstId, RemoteDMATransfer
from concourse.mybir import AluOpType as A, ActivationFunctionType as F

NR = 4
NCORES = 48
RNG = 16384
ZC = 16385
FILL = 16392
WIN = 17536
F0 = 1024

SCRATCH = {}
for _names, _w, _dt in (("win", WIN, "bfloat16"), ("kbi", 256, "int32"), ("kh kl", 64, "int32"), ("kn jt", 64, "float32"),
                        ("ko", 64, "uint16"), ("kai", 64, "int32"), ("ka1", 64, "float32"), ("qm qx", 256, "uint16"),
                        ("pidx", 1, "int32"), ("ci", 8, "int32"), ("cf at bias", 8, "float32"), ("col", 16, "float32"),
                        ("bt", 256, "bfloat16"), ("dat", 1024, "bfloat16"), ("j16 xx", 512, "float32"),
                        ("m16", 512, "bfloat16"), ("wsel", 8, "bfloat16"), ("got", 4096, "bfloat16"),
                        ("wb wv ff pd selr", 32, "float32"), ("pin", 96, "float32"), ("cii", 32, "int32"),
                        ("cidx so", 32, "uint16"), ("k32 kk pmt fn cn kf", 32, "bfloat16"),
                        ("rj pj mask8 r16 pi pm xm", 128, "float32"),
                        ("blk nblk upp eye dgo", 128, "bfloat16"), ("selh", 256, "float32"), ("w2", 2048, "float32"),
                        ("tl", 128, "uint16"), ("tabs", 4096, "float32"),
                        ("snd", 2048, "float32"), ("land", 2056, "float32"), ("fl", 64, "uint16"), ("ys", 1024, "float32")):
    for _n in _names.split():
        SCRATCH[_n] = ("sbuf", [128, _w], _dt)
for _n in ("psw", "pso", "psx", "psl", "psf"):
    SCRATCH[_n] = ("psum", [128, 512], "float32")
NEV = 128
SEMAPHORES = ["e%d" % i for i in range(NEV)] + [k + str(i) for k in ("rq", "rp", "rd") for i in range(NR)] + [
    "kq", "qr", "pp", "lk", "lq", "lr", "lp", "ld", "lw"]


def event(sem=None, total=0):
    return {"sem": sem, "total": total, "used": False, "known": []}


def run_schedule(ops, queues, T):
    know = {q: [] for q in queues}
    plan = []
    for op in ops:
        kn = know[op["q"]]
        waits = []
        for d in op["deps"]:
            if any(d is k for k in kn):
                continue
            waits.append(d)
            d["used"] = True
            for k in [d] + d["known"]:
                if not any(k is x for x in kn):
                    kn.append(k)
        if op["ev"] is not None:
            op["ev"]["known"].extend(kn)
            op["ev"]["total"] += op["n"]
        plan.append(waits)
    n = 0
    for op in ops:
        ev = op["ev"]
        if ev is not None and ev["used"] and ev["sem"] is None:
            ev["sem"] = T.sem["e%d" % n]
            n += 1
    for op, waits in zip(ops, plan):
        for d in waits:
            queues[op["q"]].wait_ge(d["sem"], d["total"])
        if op["fn"] is None:
            continue
        ins = op["fn"]()
        if op["ev"] is not None and op["ev"]["used"]:
            ins.then_inc(op["ev"]["sem"], op["n"])


def bits(m):
    return bin(m).count("1")


def low_bits(m, lo, hi):
    e = [i for i in range(m.bit_length()) if m >> i & 1]
    return sum(1 << i for i in e[lo:hi])


def rank_program(g, core, T, topo):
    team = None
    for r in range(NR):
        c0 = T.cores[r]
        if topo.chip(core) == topo.chip(c0) and topo.die(core) == topo.die(c0):
            s, team = r, [c0] + [c for c in range(NCORES) if c != c0 and topo.chip(c) == topo.chip(c0) and topo.die(c) == topo.die(c0)]
    if team is None:
        return
    part = team.index(core)
    rank = part == 0
    V, S = g.vector, g.scalar
    ops = []

    def do(q, fn, deps=(), ev=None, n=1):
        e = ev if ev is not None else event()
        ops.append({"q": q, "fn": fn, "deps": list(deps), "ev": e, "n": n})
        return e

    def plain(q, fn, deps=()):
        ops.append({"q": q, "fn": fn, "deps": list(deps), "ev": None, "n": 0})

    def act(out, in_, func, bias=0.0, scale=1.0, deps=(), ev=None):
        return do("s", lambda: S.activation(out, in_, func, bias=bias, scale=scale), deps, ev)

    def ts(out, in0, s1, s2, op0, op1=None, deps=(), ev=None):
        if op1 is None:
            return do("v", lambda: V.tensor_scalar(out, in0, s1, None, op0), deps, ev)
        return do("v", lambda: V.tensor_scalar(out, in0, s1, s2, op0, op1), deps, ev)

    def tt(out, a, b, op, deps=()):
        return do("v", lambda: V.tensor_tensor(out, a, b, op), deps)

    def vcopy(out, in_, deps=(), ev=None):
        return do("v", lambda: V.tensor_copy(out, in_), deps, ev)

    def fill(ap, deps=(), ev=None):
        return do("v", lambda: V.memset(ap, 0.0), deps, ev)

    def iota(out, pattern, base, cm, integer=False, ev=None):
        if integer:
            return do("g", lambda: g.iota(out, pattern, base, cm), (), ev)
        return do("g", lambda: g.iota(out, pattern, base, cm, allow_small_or_imprecise_dtypes=True), (), ev)

    def mm(out, lhsT, rhs, start, stop, deps=(), ev=None):
        return do("t", lambda: g.tensor.matmul(out, lhsT, rhs, start, stop), deps, ev)

    def dma(out, in_, deps=(), ev=None, q="y"):
        return do(q, lambda: (S if q == "s" else g.sync).dma_start(out, in_), deps, ev, 16)

    def fused(tr, lsem, deps):
        def issue():
            xs = []
            for m, rsem, src, dst, cores in tr:
                ids = [topo.addr(c) for c in cores]
                xs.append(RemoteDMATransfer(dst_ids=[DstId(rid=i[0], pnc=i[1]) for i in ids], dma_engine_mask=m,
                                            remote_sem=rsem, srcs=[src], dsts=[dst for _ in cores]))
            return g.remote_dma_fused(xs, local_sem=lsem)
        plain("g", issue, deps)

    if rank:
        peers = [r for r in range(NR) if r != s]
        far = [r for r in peers if topo.chip(T.cores[r]) != topo.chip(core)]
        near = [r for r in peers if topo.chip(T.cores[r]) == topo.chip(core)]
        assert all(topo.may_write(core, T.cores[r]) for r in peers)
        fmask = topo.mask(core, T.cores[far[0]])
        nmask = topo.mask(core, T.cores[near[0]]) & ~fmask
        nin = {r: bits(fmask if r in far else nmask) for r in peers}

        def share(ap, rsem, lsem, deps):
            fused([(m, rsem, ap, ap, [T.cores[r] for r in rs]) for rs, m in ((far, fmask), (near, nmask))], lsem, deps)
    tmask = topo.mask(team[0], team[1])

    e_kb, e_ka = event(), event()
    if rank:
        for t, src, ev in ((T.kbi, T.kb, e_kb), (T.kai, T.ka, e_ka)):
            for gr in range(8):
                dma(t[16 * gr:16 * gr + 16, :], src[:, :], ev=ev, q="ys"[gr % 2])
    else:
        e_kb = event(T.sem.kq, 4)

    f_0 = fill(T.win[:, 0:F0])
    i_p = iota(T.pidx[:], [[0, 1]], 0, 1, True)
    i_a = iota(T.at[:, 0:4], [[1, 4]], 1 + 4 * part, 0)
    i_j = iota(T.jt[:], [[16, 64]], ZC, 1)
    i_b = iota(T.bt[:], [[1, 256]], 1, 0)
    if rank:
        fused([(low_bits(tmask, 4 * j - 4, 4 * j), T.sem.kq, T.kbi[:, 64 * j:64 * j + 64], T.kbi[:, 0:64], [team[j]]) for j in (1, 2, 3)],
              T.sem.lk, [e_kb])

    F1 = F0 + (7 if rank else 5) * F0
    F2 = F1 + (1 if rank else 3) * F0
    F3 = F2 + 2 * F0
    f_d, f_a, f_g, f_v = event(), event(), event(), event()
    for c in range(F1, F2, F0):
        dma(T.win[:, c:c + F0], T.win[:, 0:F0], [f_0], f_d)
    for c in range(F0, F1, F0):
        act(T.win[:, c:c + F0], T.win[:, 0:F0], F.Copy, deps=[f_0], ev=f_a)
    vb = [F3 + 8 * ((FILL - F3) // 8 * k // 4) for k in range(4)] + [FILL]

    def vfill(k):
        fill(T.win[:, vb[k]:vb[k + 1]], ev=f_v)

    def gfill(k):
        iota(T.win[:, F2 + F0 * k:F2 + F0 * k + F0], [[0, F0]], 0, 0, ev=f_g)

    LANE, GRP, ODD, RQ, H = range(5)
    QM1, EV, ORDP, WT, W0, W1 = range(6)
    SH, AND, SUB = A.arith_shift_right, A.bitwise_and, A.subtract
    e_c = event()
    for k, a, b, o1, o2 in ((GRP, 4, None, SH, None), (LANE, 15, None, AND, None), (ODD, 1, None, AND, None),
                            (RQ, 4, 3, SH, AND), (H, 6, None, SH, None)):
        ts(T.ci[:, k:k + 1], T.pidx[:], a, b, o1, o2, [i_p], e_c)
    if not rank:
        vfill(0)
    e_cf = vcopy(T.cf[:, 0:5], T.ci[:, 0:5], [e_c])

    def fc(k):
        return T.cf[:, k:k + 1]

    def cc(k):
        return T.col[:, k:k + 1]

    e_qm = ts(cc(QM1), fc(GRP), float(RNG), -1.0, A.mult, A.add, [e_cf])
    e_ev = ts(cc(EV), fc(ODD), -1.0, 1.0, A.mult, A.add, [e_cf])
    e_bias = ts(T.bias[:, 0:4], T.at[:, 0:4], fc(ODD), None, A.mult, deps=[e_cf, i_a])
    if rank:
        qlo = T.qm[:, 64 * s:64 * s + 64]
        e = ts(T.ka1[:], T.kai[:], cc(QM1), 0.0, SUB, A.max, [e_ka, e_qm])
        e_ql = ts(qlo, T.ka1[:], float(ZC), None, A.min, deps=[e])
        share(qlo, T.sem["rq%d" % s], T.sem.lq, [e_ql])
        q_in = {r: event(T.sem["rq%d" % r], nin[r]) for r in peers}
        q_in[s] = e_ql
    else:
        vfill(1)
        gfill(1)
    gfill(0)

    e_dat = event()
    for a in range(4):
        ts(T.dat[:, 256 * a:256 * a + 256], T.bt[:], cc(EV), T.bias[:, a:a + 1], A.mult, A.add, [e_ev, e_bias, i_b], e_dat)
    if rank:
        vfill(0)
        vfill(1)
        e_q = [vcopy(T.qx[:, r::4], T.qm[:, 64 * r:64 * r + 64], [q_in[r]]) for r in [s] + near + far]
        fused([(tmask, T.sem.qr, T.qx[:], T.qx[:], team[1:])], T.sem.lr, e_q)
        e_lr = event(T.sem.lr, bits(tmask))
        e_tab = dma(T.tabs[:, :], T.tab[:, :], [e_lr])
        gfill(1)
    else:
        e_q = [event(T.sem.qr, bits(tmask))]
        vfill(2)
        vfill(3)
    e1 = ts(T.kh[:], T.kbi[:, 0:64], 14, None, SH, deps=[e_kb])
    e2 = ts(T.kl[:], T.kbi[:, 0:64], RNG - 1, None, AND, deps=[e_kb])
    e = ts(T.kn[:], T.kh[:], fc(GRP), None, A.not_equal, deps=[e1, e_cf])
    if rank:
        vfill(2)
    e = tt(T.kn[:], T.kn[:], T.jt[:], A.mult, [e, i_j])
    if rank:
        vfill(3)
    e = tt(T.kn[:], T.kn[:], T.kl[:], A.max, [e, e2])
    e_ko = ts(T.ko[:], T.kn[:], 1.0, None, A.add, deps=[e])
    e_dir = vcopy(T.win[:, 0:WIN].indirect(T.ko[:, 0:64]), T.dat[:], [f_0, f_d, f_g, f_v, f_a, e_ko, e_dat])

    e = act(cc(WT), fc(LANE), F.Abs, -1.0, 1.0, [e_cf])
    e0 = act(cc(W0), fc(LANE), F.Relu, 1.0, -1.0, [e_cf])
    e1 = act(cc(W1), cc(WT), F.Relu, 256.0, -256.0, [e])
    e_ws = act(T.wsel[:, 0:1], cc(W0), F.Identity, cc(W1), 1.0, [e0, e1])

    if rank:
        i_16 = iota(T.j16[:], [[0, 32], [1, 16]], 0, 0)
        i_rj = iota(T.rj[:], [[0, 2], [1, 4], [0, 16]], 0, 0)
        i_pj = iota(T.pj[:], [[-1, 128]], 0, 1)
        i_k = iota(T.k32[:], [[32, 32]], 0, 0)
        i_kk = iota(T.kk[:], [[32, 32]], 512, 0)
        e = act(T.j16[:], T.j16[:], F.Abs, fc(LANE), -1.0, [i_16, e_cf])
        e_m16 = act(T.m16[:], T.j16[:], F.Relu, 1.0, -1.0, [e])
        e = act(T.rj[:], T.rj[:], F.Abs, fc(RQ), -1.0, [i_rj, e_cf])
        e_op = act(cc(ORDP), fc(H), F.Identity, fc(LANE), 16.0, [e_cf])
        e_bl = act(T.blk[:], T.rj[:], F.Relu, 1.0, -1.0, [e])
        e = act(T.pj[:], T.pj[:], F.Abs, deps=[i_pj])
        e_nb = act(T.nblk[:], T.blk[:], F.Copy, 0.0, -1.0, [e_bl])
        e_eye = act(T.eye[:], T.pj[:], F.Relu, 1.0, -1.0, [e])
        e_pt = act(T.pmt[:], T.k32[:], F.Identity, cc(ORDP), 0.0, [i_k, e_op])
        e_dg = act(T.dgo[:], T.eye[:], F.Copy, 0.0, cc(ORDP), [e_eye, e_op])
        i_ci = iota(T.cii[:], [[1, 32]], 0, 0, True)
        z_w2 = iota(T.w2[:, 0:512], [[0, 512]], 0, 0)
        e_up = do("g", lambda: g.affine_select(T.upp[:], T.blk[:], [[-1, 128]], A.is_ge, 0.0, 0, 1), [e_bl])
        i_r = iota(T.selr[:], [[0, 8], [1, 4]], 0, 0)
        i_bi = iota(T.mask8[:], [[0, 4], [1, 8], [0, 4]], 0, 0)
        i_i = iota(T.r16[:], [[0, 8], [1, 16]], 0, 0)
        i_pi = iota(T.pi[:], [[0, 8], [-1, 16]], 0, 1)

    e_w = [event(), event()]
    half = [T.psw, T.psw if rank else T.psx]

    def partial(b):
        e = vcopy(T.wb[:, 16 * b:16 * b + 16], half[b][:, 16 * b:16 * b + 16], [e_w[b]])
        rid, pid, _ = topo.addr(team[0])
        m = low_bits(topo.mask(core, team[0]), 0, 8)
        plain("g", lambda: g.remote_dma(T.pin[:, 32 * part - 32 + 16 * b:32 * part - 16 + 16 * b], T.wb[:, 16 * b:16 * b + 16],
                                        T.sem.pp, T.sem.lw, pid=pid, routing_id=rid, dma_engine_mask=m), [e])

    for n in range(8):
        win = T.win[:, 0:ZC + 1].indirect(T.qx[:, 32 * n:32 * n + 32])
        o = T.got[:, 512 * n:512 * n + 512]
        dep = [e_dir] + e_q
        e = vcopy(o, win, dep) if n % 2 == 0 else act(o, win, F.Copy, deps=dep)
        for k in range(4 * n, 4 * n + 4):
            mm(half[n // 4][:, k:k + 1], T.got[:, 128 * k:128 * k + 128], T.wsel[:, 0:1], True, True, [e, e_ws], e_w[n // 4])
        if n == 4 and not rank:
            partial(0)

    queues = {"g": g, "v": V, "s": S, "y": g.sync, "t": g.tensor}
    if not rank:
        partial(1)
        plain("g", None, [event(T.sem.lw, 16)])
        run_schedule(ops, queues, T)
        return

    e = act(T.selr[:], T.selr[:], F.Abs, fc(RQ), -1.0, [i_r])
    e_bi = act(T.mask8[:], T.mask8[:], F.Abs, fc(GRP), -1.0, [i_bi])
    e_ii = act(T.r16[:], T.r16[:], F.Abs, fc(LANE), -1.0, [i_i])
    e_selr = act(T.selr[:], T.selr[:], F.Relu, 1.0, -1.0, [e])
    e_m8 = act(T.mask8[:], T.mask8[:], F.Relu, 1.0, -1.0, [e_bi])
    e_r16 = act(T.r16[:], T.r16[:], F.Relu, 1.0, -1.0, [e_ii])
    po = T.pso[:, 0:32]
    mm(po, T.eye[:], T.k32[:], True, False, [e_eye, i_k])
    mm(po, T.eye[:], T.pmt[:], False, False, [e_pt])
    z_ld = fill(T.land[:, 2048:2056])
    e_ci = vcopy(T.cidx[:], T.cii[:], [i_ci])
    e_sh = event()
    for h in range(2):
        ts(T.selh[:, 128 * h:128 * h + 128], T.pi[:], float(16 * (4 * h + s)), None, A.is_equal, deps=[i_pi], ev=e_sh)

    e_pp = event(T.sem.pp, 3 * 2 * 8)
    eb = tt(T.wb[:], T.pin[:, 32:64], T.pin[:, 64:96], A.add, [e_pp])
    ea = tt(T.wv[:], T.psw[:, 0:32], T.pin[:, 0:32], A.add, [e_pp] + e_w)
    e_wv = tt(T.wv[:], T.wv[:], T.wb[:], A.add, [ea, eb])
    e_fn = ts(T.fn[:], T.wv[:], 0.0, None, A.is_equal, deps=[e_wv])
    e_cn = do("v", lambda: V.tensor_tensor_scan(T.cn[:], T.fn[:], T.fn[:], 0.0, A.add, A.max), [e_fn])
    e_kf = tt(T.kf[:], T.kk[:], T.fn[:], A.mult, [i_kk, e_fn])
    e_x = tt(T.xx[:], T.wv[:, 0:32].indirect(T.cidx[:, 0:32]), T.m16[:], A.mult, [e_wv, e_ci, e_m16])
    mm(po, T.dgo[:], T.fn[:], False, False, [e_dg, e_fn])
    mm(po, T.upp[:], T.fn[:], False, False, [e_up])
    mm(po, T.nblk[:], T.cn[:], False, False, [e_nb, e_cn])
    e_z = mm(po, T.eye[:], T.kf[:], False, True, [e_kf])
    e_so = vcopy(T.so[:], po, [e_z])
    e_ff = ts(T.ff[:], T.fn[:], -1.0, 1.0, A.mult, A.add, [e_fn])
    e_w2 = vcopy(T.w2[:, 0:2048].indirect(T.so[:, 0:32]), T.xx[:], [e_so, e_x, z_w2])
    e = ts(T.pd[:], T.so[:], float(512 * s - 2048), None, A.add, deps=[e_so])
    pmo = T.pm[:, 32 * s:32 * s + 32]
    e_pm = tt(pmo, T.pd[:], T.ff[:], A.mult, [e, e_ff])
    share(pmo, T.sem["rp%d" % s], T.sem.lp, [e_pm])
    e_x = event()
    for k in range(4):
        mm(T.psx[:, 32 * k:32 * k + 32], T.w2[:, 128 * k:128 * k + 128], T.selr[:], True, True, [e_w2, e_selr], e_x)
    e = tt(T.xm[:], T.psx[:, 0:128], T.mask8[:], A.mult, [e_x, e_m8])
    places = ((far[0], T.psl, 0), (far[1], T.psw, 0), (near[0], T.pso, 32), (s, T.pso, 64))
    e_l = {}
    for r, ps, c in places:
        e_l[r] = mm(ps[:, c:c + 32], T.r16[:], T.xm[:, r::4], True, True, [e, e_r16])

    land = T.land[:, 512 * s:512 * s + 512]
    e_col = {}
    for r, ps, c in places:
        dep = [e_l[r]] if r in far else [e_l[near[0]], e_l[s]]
        e_tl = ts(T.tl[:, 32 * r:32 * r + 32], ps[:, c:c + 32], -257.0, 0.0, A.add, A.max, dep)
        e_col[r] = event()
        buf = T.land if r == s else T.snd
        for h in range(2):
            w = T.tabs[:, :].indirect(T.tl[:, 32 * r + 16 * h:32 * r + 16 * h + 16])
            o = buf[:, 512 * r + 256 * h:512 * r + 256 * h + 256]
            if h == 0:
                vcopy(o, w, [e_tl, e_tab], e_col[r])
            else:
                act(o, w, F.Copy, deps=[e_tl, e_tab], ev=e_col[r])
    for r in far + near:
        rid, pid, _ = topo.addr(T.cores[r])
        plain("g", lambda r=r, rid=rid, pid=pid: g.remote_dma(
            land, T.snd[:, 512 * r:512 * r + 512], T.sem["rd%d" % s], T.sem.ld, pid=pid, routing_id=rid,
            dma_engine_mask=fmask if r in far else nmask), [e_col[r]])

    order = [s] + near + far
    p_in = {r: event(T.sem["rp%d" % r], nin[r]) for r in peers}
    p_in[s] = e_pm
    e_f = []
    for h in range(2):
        for n, r in enumerate(order):
            e = mm(T.psf[:, 32 * h:32 * h + 32], T.selh[:, 128 * h:128 * h + 128], T.pm[:, 32 * r:32 * r + 32], n == 0, n == 3, [e_sh, p_in[r]])
        e_f.append(e)
    e_fl = [ts(T.fl[:, h::2], T.psf[:, 32 * h:32 * h + 32], 2048.0, None, A.add, deps=e_f) for h in range(2)]
    d_in = [event(T.sem["rd%d" % r], nin[r]) for r in peers]
    e_y = event()
    for k in range(4):
        w = T.land[:, 0:2049].indirect(T.fl[:, 16 * k:16 * k + 16])
        o = T.ys[:, 256 * k:256 * k + 256]
        dep = e_fl + [e_col[s], z_ld] + d_in
        e = vcopy(o, w, dep) if k % 2 == 0 else act(o, w, F.Copy, deps=dep)
        dma(T.y[:, 256 * k:256 * k + 256], o, [e], e_y)
    plain("y", None, [e_y])
    n = bits(fmask) + bits(nmask)
    plain("g", None, [event(T.sem.lk, 12), event(T.sem.lq, n), e_lr, event(T.sem.lp, n), event(T.sem.ld, n + bits(fmask))])
    run_schedule(ops, queues, T)
